import numpy as np
import ml_dtypes


def mxq(x, axis, fmt="e4m3"):
    dtype, down = {"e4m3": (ml_dtypes.float8_e4m3fn, 7), "e5m2": (ml_dtypes.float8_e5m2, 14)}[fmt]
    v = np.moveaxis(np.asarray(x, np.float32).astype(ml_dtypes.bfloat16).astype(np.float64), axis, -1)
    blocks = v.reshape(v.shape[:-1] + (-1, 32))
    amax = np.abs(blocks).max(-1, keepdims=True)
    byte = np.maximum(np.where(amax > 0, np.frexp(amax)[1] - 1 + 127, 0) - down, 1)
    scale = np.exp2(byte - 127.0)
    codes = (blocks / scale).astype(np.float32).astype(dtype).astype(np.float64)
    return np.moveaxis((codes * scale).reshape(v.shape), -1, axis)


WIDE = False


def mx_kscale(k):
    if not WIDE:
        return np.ones(k)
    levels = np.array([10, -10, 5, -5, 0])
    if k % 512:
        return np.exp2(np.random.permutation(np.resize(levels, k // 32))).repeat(32)
    a = np.empty((k // 512, 16))
    for p in range(k // 512):
        a[p, :8] = np.random.permutation(np.resize(levels, 8))
        for g in range(8):
            far = levels[np.abs(levels - a[p, g]) >= 10]
            a[p, g + 8] = far[np.random.randint(len(far))]
    return np.exp2(a.ravel()).repeat(32)


def f64(x):
    return np.asarray(x).astype(np.float64)


def striped(idx):
    return np.tile(np.asarray(idx).reshape(-1, 16).T, (8, 1)).astype(np.uint16)


def unstriped(offs):
    return offs[:16].T.reshape(-1).astype(np.int64)


def gelu(v):
    return 0.5 * v * (1.0 + np.tanh(0.7978845608028654 * (v + 0.044715 * v ** 3)))


def bf(x):
    return np.asarray(x, np.float32).astype(ml_dtypes.bfloat16)


def planes(Y):
    r, m = Y.shape
    b = f64(bf(Y)).reshape(r // 32, 32, m)
    amax = np.abs(b).max(1)
    byte = np.clip(np.where(amax > 0, np.frexp(amax)[1] - 1 + 127 - 7, 1), 1, 254)
    codes = (b * np.exp2(127.0 - byte)[:, None, :]).reshape(r, m).astype(np.float32).astype(ml_dtypes.float8_e4m3fn).view(np.uint8)
    words = codes.reshape(r // 512, 128, 4, m).transpose(0, 1, 3, 2)
    return np.ascontiguousarray(words), np.ascontiguousarray(byte.astype(np.uint8).reshape(r // 512, 16, m))


E, T, I, F, J = 512, 2048, 512, 512, 512


def setup_inputs():
    n = np.random.standard_normal
    idx = np.random.permutation(T)[:I]
    fi = mx_kscale(I)
    ff = mx_kscale(F)
    ti = np.ones(T)
    ti[idx] = fi
    return {
        "tok": (n((E, T)) / ti).astype(np.float32),
        "wa": (n((I, F)) * 1 / np.sqrt(I) * fi[:, None]).astype(np.float32),
        "gain": (np.random.uniform(0.5, 2.0, (F, 1)) * ff[:, None]).astype(np.float32),
        "wb": (n((F, J)) * 1 / np.sqrt(F) / ff[:, None]).astype(np.float32),
        "offs": striped(idx),
    }


def reference(tok, wa, gain, wb, offs):
    idx = unstriped(offs)
    xt = f64(tok)[:, idx].T
    waq = mxq(f64(wa), 0, "e4m3")
    xtq = mxq(xt, 0, "e4m3")
    z = waq.T @ xtq
    g = gelu(z) * f64(gain)
    wbq = mxq(f64(wb), 0, "e4m3")
    gq = mxq(g, 0, "e4m3")
    y = wbq.T @ gq
    words, scales = planes(y)
    return y, words, scales

@@ -1,0 +1,227 @@
+from contextlib import ExitStack
+
+import concourse.mybir as mybir
+from concourse.masks import make_identity
+
+E, T, K = 512, 2048, 512
+FLOPS = 2 * 2 * 512 * 512 * 512
+
+F32 = mybir.dt.float32
+BF16 = mybir.dt.bfloat16
+I32 = mybir.dt.int32
+U32 = mybir.dt.uint32
+U16 = mybir.dt.uint16
+U8 = mybir.dt.uint8
+FP8X4 = mybir.dt.float8_e4m3fn_x4
+GELU = mybir.ActivationFunctionType.Gelu_apprx_tanh
+MULT = mybir.AluOpType.mult
+
+P = 128
+PACK = 4
+HALF = P // 2
+BLOCKS = E // P
+PLACE = {"window0":0,"window1":8192,"window2":16384,"window3":24576,"wa_raw":32768,"wb_raw0":40960,"wa":0,"xt0":4096,"xt0_codes":32768,"picked1":3584,"g0":8192,"xt1":49152,"picked2":48640,"wb_raw1":61440,"wb":45056,"picked3":16384,"g1":24576,"xt2_codes":25600,"xt3":40960,"xt3_codes":61440,"wb_codes":40960,"g2":45056,"g3":57344,"y_bf01":57344,"act2":43008}
+BANK = {"turned0":0,"z0":1,"turned1":2,"z1":3,"turned2":0,"turned3":2,"z2":1,"z3":3,"y01_0":4,"y01_1":5,"y2":6,"y3":7}
+
+
+def tile_attend_tokenmixer_pl_kernel(tc, tok, wa, gain, wb, offs, out_0, out_1, out_2):
+    nc = tc.nc
+    with ExitStack() as ctx:
+        keep = ctx.enter_context(tc.tile_pool(name="keep", bufs=1))
+        stage = ctx.enter_context(tc.tile_pool(name="stage", bufs=1))
+        psum = ctx.enter_context(tc.psum_pool(name="psum", bufs=1))
+
+        def staged(name, shape, dtype):
+            if name in PLACE:
+                return stage.tile(shape, dtype, name=name, align_bytes=64, offset=PLACE[name])
+            return keep.tile(shape, dtype, name=name, align_bytes=64)
+
+        def bank(name, shape):
+            return psum.tile(shape, F32, name=name, offset=2048 * BANK[name])
+
+        offsets = keep.tile([P, K // 16], U16, name="offsets")
+        gain_sb = keep.tile([P, 1, PACK], F32, name="gain_sb")
+        window = [staged("window%d" % b, [P, T], F32) for b in range(BLOCKS)]
+        wa_raw = staged("wa_raw", [P, PACK, K], F32)
+        wb_raw = [staged("wb_raw%d" % h, [P, PACK, K // 2], F32) for h in range(2)]
+
+        nc.sync.dma_start(offsets[:], offs)
+        nc.sync.dma_start(window[0][:], tok[0:P, :])
+        nc.sync.dma_start(wa_raw[:], wa.rearrange("(p s) c -> p s c", s=PACK))
+        nc.sync.dma_start(gain_sb[:], gain.rearrange("(p t) o -> p o t", t=PACK))
+        for b in range(1, BLOCKS):
+            nc.sync.dma_start(window[b][:], tok[b * P : (b + 1) * P, :])
+        wb_rows = wb.rearrange("(p s) c -> p s c", s=PACK)
+        for h in range(2):
+            nc.sync.dma_start(wb_raw[h][:], wb_rows[:, :, h * K // 2 : (h + 1) * K // 2])
+
+        identity = keep.tile([P, P], F32, name="identity")
+        make_identity(nc, identity[:])
+
+        def operand(name, width):
+            return staged(name + "_codes", [P, width], U32), staged(name + "_scales", [P, width], U8)
+
+        def quantise_into(target, cols, values):
+            nc.vector.quantize_mx(
+                out=target[0][:, cols].bitcast(FP8X4), scales=target[1][:, cols], in_=values
+            )
+
+        def quantise(name, values):
+            width = values.shape[1] // PACK
+            target = operand(name, width)
+            quantise_into(target, slice(0, width), values[:])
+            return target
+
+        def deal(name, raw, copy):
+            dealt = staged(name, [P, PACK * raw.shape[2]], BF16)
+            copy(
+                dealt[:].rearrange("p (t m s) -> p m s t", t=PACK, s=PACK),
+                raw[:].rearrange("p s (m t) -> p m s t", t=PACK),
+            )
+            return dealt
+
+        def deal_half(dealt, h, copy):
+            copy(
+                dealt[:].rearrange("p (t m s) -> p m s t", t=PACK, s=PACK)[:, h * HALF : (h + 1) * HALF],
+                wb_raw[h][:].rearrange("p s (m t) -> p m s t", t=PACK),
+            )
+
+        def quantise_half(target, h, dealt):
+            for t in range(PACK):
+                first = t * P + h * HALF
+                quantise_into(
+                    target, slice(first, first + HALF), dealt[:, t * PACK * HALF : (t + 1) * PACK * HALF]
+                )
+
+        def product(name, weights, moving):
+            sums = bank(name, [P, PACK, P])
+            for t in range(PACK):
+                cols = slice(t * P, (t + 1) * P)
+                nc.tensor.matmul_mx(
+                    out=sums[:, t, :],
+                    lhsT=weights[0][:, cols].bitcast(FP8X4),
+                    lhsT_scale=weights[1][:, cols],
+                    rhs=moving[0][:].bitcast(FP8X4),
+                    rhs_scale=moving[1][:],
+                    start=True,
+                    stop=True,
+                )
+            return sums
+
+        def tokens(b):
+            picked = staged("picked%d" % b, [P, K], BF16)
+            nc.vector.tensor_copy(picked[:], window[b][:].indirect(offsets[:]))
+            words = picked[:].bitcast(F32)
+            turned = bank("turned%d" % b, [P, 2, P])
+            for u in range(2):
+                nc.tensor.transpose(turned[:, u, :], words[:, u : K // 2 : 2], identity[:])
+            xt = staged("xt%d" % b, [P, P * PACK], BF16)
+            nc.scalar.copy(
+                xt[:].bitcast(F32).rearrange("p (e u) -> p e u", u=2),
+                turned[:].rearrange("p u e -> p e u"),
+            )
+            return xt
+
+        def hidden(b, wa_q, xt_q):
+            z = product("z%d" % b, wa_q, xt_q)
+            act = staged("act%d" % b, [P, P, PACK], F32)
+            nc.scalar.activation(act[:], z[:].rearrange("p t e -> p e t"), GELU)
+            return act
+
+        def gained(b, act):
+            g = staged("g%d" % b, [P, P * PACK], BF16)
+            nc.vector.tensor_tensor(
+                g[:].rearrange("p (e t) -> p e t", t=PACK),
+                act[:],
+                gain_sb[:].to_broadcast([P, P, PACK]),
+                MULT,
+            )
+            return g
+
+        def product_pair(weights, moving):
+            banks = [bank("y01_%d" % a, [P, 2, 2 * P]) for a in range(2)]
+            for t in range(PACK):
+                cols = slice(t * P, (t + 1) * P)
+                nc.tensor.matmul_mx(
+                    out=banks[t // 2][:, t % 2, :],
+                    lhsT=weights[0][:, cols].bitcast(FP8X4),
+                    lhsT_scale=weights[1][:, cols],
+                    rhs=moving[0][:].bitcast(FP8X4),
+                    rhs_scale=moving[1][:],
+                    start=True,
+                    stop=True,
+                )
+            return banks
+
+        def interleave(copy, target, y):
+            copy(target.rearrange("p (e t) -> p e t", t=PACK), y[:].rearrange("p t e -> p e t"))
+
+        y_q = operand("y", E)
+        y_rows = out_0.rearrange("(p t) e -> p t e", t=PACK)
+        word_rows = out_1.rearrange("z l c r -> (z l) (c r)").bitcast(I32)
+        scale_rows = out_2.rearrange("z q c -> (z q) c").bitcast(I32)
+
+        def stored(b, y, queue):
+            y_sb = staged("y_sb%d" % b, [P, PACK, P], F32)
+            nc.scalar.copy(y_sb[:], y[:])
+            queue.dma_start(y_rows[:, :, b * P : (b + 1) * P], y_sb[:])
+            return y_sb
+
+        def rounded(b, y):
+            y_bf = staged("y_bf%d" % b, [P, P * PACK], BF16)
+            nc.vector.tensor_copy(
+                y_bf[:].rearrange("p (e t) -> p e t", t=PACK),
+                y[:].rearrange("p t e -> p e t"),
+            )
+            return y_bf
+
+        def planes(b, y_bf):
+            quantise_into(y_q, slice(b * P, (b + 1) * P), y_bf[:])
+
+        def store_words(cols):
+            nc.sync.dma_start(word_rows[:, cols], y_q[0][:, cols].bitcast(I32))
+
+        def store_scales(q, queue):
+            queue.dma_start(
+                scale_rows[4 * q : 4 * q + 4, :], y_q[1][32 * q : 32 * q + 4, :].bitcast(I32)
+            )
+
+        xt0 = tokens(0)
+        wa_bf = deal("wa", wa_raw, nc.vector.tensor_copy)
+        xt0_q = quantise("xt0", xt0)
+        wa_q = quantise("wa", wa_bf)
+        act0 = hidden(0, wa_q, xt0_q)
+        xt1 = tokens(1)
+        g01_q = operand("g01", 2 * P)
+        quantise_into(g01_q, slice(0, P), gained(0, act0)[:])
+        act1 = hidden(1, wa_q, quantise("xt1", xt1))
+        xt2 = tokens(2)
+        wb_bf = staged("wb", [P, PACK * K], BF16)
+        deal_half(wb_bf, 0, nc.scalar.copy)
+        xt3 = tokens(3)
+        g1 = gained(1, act1)
+        act2 = hidden(2, wa_q, quantise("xt2", xt2))
+        quantise_into(g01_q, slice(P, 2 * P), g1[:])
+        deal_half(wb_bf, 1, nc.vector.tensor_copy)
+        act3 = hidden(3, wa_q, quantise("xt3", xt3))
+        wb_q = quantise("wb", wb_bf)
+        y01 = product_pair(wb_q, g01_q)
+        y2 = product("y2", wb_q, quantise("g2", gained(2, act2)))
+        y3 = product("y3", wb_q, quantise("g3", gained(3, act3)))
+        y01_sb = staged("y_sb01", [P, PACK, 2 * P], F32)
+        for a in range(2):
+            nc.scalar.copy(y01_sb[:, 2 * a : 2 * a + 2, :], y01[a][:])
+        nc.sync.dma_start(y_rows[:, :, 0 : 2 * P], y01_sb[:])
+        stored(2, y2, nc.sync)
+        y01_bf = staged("y_bf01", [P, 2 * P * PACK], BF16)
+        y23_bf = staged("y_bf23", [P, 2 * P * PACK], BF16)
+        interleave(nc.vector.tensor_copy, y01_bf[:], y01_sb)
+        interleave(nc.scalar.copy, y23_bf[:, 0 : P * PACK], y2)
+        interleave(nc.vector.tensor_copy, y23_bf[:, P * PACK : 2 * P * PACK], y3)
+        stored(3, y3, nc.scalar)
+        quantise_into(y_q, slice(0, 2 * P), y01_bf[:])
+        store_words(slice(0, 2 * P))
+        quantise_into(y_q, slice(2 * P, 4 * P), y23_bf[:])
+        store_words(slice(2 * P, 4 * P))
+        for q in range(4):
+            store_scales(q, nc.sync)

@@ -20,8 +20,9 @@ P = 128
 PACK = 4
 HALF = P // 2
 BLOCKS = E // P
-PLACE = {"window0":0,"window1":8192,"window2":16384,"window3":24576,"wa_raw":32768,"wb_raw0":40960,"wa":0,"xt0":4096,"xt0_codes":32768,"picked1":3584,"g0":8192,"xt1":49152,"picked2":48640,"wb_raw1":61440,"wb":45056,"picked3":16384,"g1":24576,"xt2_codes":25600,"xt3":40960,"xt3_codes":61440,"wb_codes":40960,"g2":45056,"g3":57344,"y_bf01":57344,"act2":43008}
-BANK = {"turned0":0,"z0":1,"turned1":2,"z1":3,"turned2":0,"turned3":2,"z2":1,"z3":3,"y01_0":4,"y01_1":5,"y2":6,"y3":7}
+WB_PARTS = (slice(0, 48), slice(48, P))
+PLACE = {"window0":0,"window1":8192,"window2":16384,"window3":24576,"wa_raw":32768,"wb_raw0":40960,"wb_raw1":61440,"wa":0,"xt0_codes":32768,"picked1":3584,"g0":8192,"xt1":49152,"picked2":48640,"picked3":49664,"wb":45056,"g1":24576,"xt2_codes":25600,"xt3":40960,"act2":41984,"xt3_codes":61440,"g2":62464,"g3":57344,"y_bf01":57344,"xt0":4096}
+BANK = {"turned0":0,"z0":1,"turned1":2,"z1":3,"turned2":0,"turned3":2,"z2":1,"z3":3,"y01_0":4,"y01_1":5,"y2":6,"y3_0":7,"y3_1":0}
 
 
 def tile_attend_tokenmixer_pl_kernel(tc, tok, wa, gain, wb, offs, out_0, out_1, out_2):
@@ -43,17 +44,17 @@ def tile_attend_tokenmixer_pl_kernel(tc, tok, wa, gain, wb, offs, out_0, out_1, 
         gain_sb = keep.tile([P, 1, PACK], F32, name="gain_sb")
         window = [staged("window%d" % b, [P, T], F32) for b in range(BLOCKS)]
         wa_raw = staged("wa_raw", [P, PACK, K], F32)
-        wb_raw = [staged("wb_raw%d" % h, [P, PACK, K // 2], F32) for h in range(2)]
+        wb_raw = [staged("wb_raw%d" % h, [P, PACK, PACK * (WB_PARTS[h].stop - WB_PARTS[h].start)], F32) for h in range(2)]
 
-        nc.sync.dma_start(offsets[:], offs)
         nc.sync.dma_start(window[0][:], tok[0:P, :])
+        nc.sync.dma_start(offsets[:], offs)
         nc.sync.dma_start(wa_raw[:], wa.rearrange("(p s) c -> p s c", s=PACK))
-        nc.sync.dma_start(gain_sb[:], gain.rearrange("(p t) o -> p o t", t=PACK))
+        nc.scalar.dma_start(gain_sb[:], gain.rearrange("(p t) o -> p o t", t=PACK))
         for b in range(1, BLOCKS):
             nc.sync.dma_start(window[b][:], tok[b * P : (b + 1) * P, :])
         wb_rows = wb.rearrange("(p s) c -> p s c", s=PACK)
         for h in range(2):
-            nc.sync.dma_start(wb_raw[h][:], wb_rows[:, :, h * K // 2 : (h + 1) * K // 2])
+            nc.sync.dma_start(wb_raw[h][:], wb_rows[:, :, PACK * WB_PARTS[h].start : PACK * WB_PARTS[h].stop])
 
         identity = keep.tile([P, P], F32, name="identity")
         make_identity(nc, identity[:])
@@ -80,9 +81,9 @@ def tile_attend_tokenmixer_pl_kernel(tc, tok, wa, gain, wb, offs, out_0, out_1, 
             )
             return dealt
 
-        def deal_half(dealt, h, copy):
+        def deal_part(dealt, h, copy):
             copy(
-                dealt[:].rearrange("p (t m s) -> p m s t", t=PACK, s=PACK)[:, h * HALF : (h + 1) * HALF],
+                dealt[:].rearrange("p (t m s) -> p m s t", t=PACK, s=PACK)[:, WB_PARTS[h]],
                 wb_raw[h][:].rearrange("p s (m t) -> p m s t", t=PACK),
             )
 
@@ -138,8 +139,8 @@ def tile_attend_tokenmixer_pl_kernel(tc, tok, wa, gain, wb, offs, out_0, out_1, 
             )
             return g
 
-        def product_pair(weights, moving):
-            banks = [bank("y01_%d" % a, [P, 2, 2 * P]) for a in range(2)]
+        def product_halves(name, weights, moving, width):
+            banks = [bank("%s_%d" % (name, a), [P, 2, width]) for a in range(2)]
             for t in range(PACK):
                 cols = slice(t * P, (t + 1) * P)
                 nc.tensor.matmul_mx(
@@ -187,41 +188,42 @@ def tile_attend_tokenmixer_pl_kernel(tc, tok, wa, gain, wb, offs, out_0, out_1, 
             )
 
         xt0 = tokens(0)
-        wa_bf = deal("wa", wa_raw, nc.vector.tensor_copy)
-        xt0_q = quantise("xt0", xt0)
-        wa_q = quantise("wa", wa_bf)
-        act0 = hidden(0, wa_q, xt0_q)
+        wa_q = quantise("wa", deal("wa", wa_raw, nc.vector.tensor_copy))
+        act0 = hidden(0, wa_q, quantise("xt0", xt0))
         xt1 = tokens(1)
         g01_q = operand("g01", 2 * P)
         quantise_into(g01_q, slice(0, P), gained(0, act0)[:])
         act1 = hidden(1, wa_q, quantise("xt1", xt1))
         xt2 = tokens(2)
         wb_bf = staged("wb", [P, PACK * K], BF16)
-        deal_half(wb_bf, 0, nc.scalar.copy)
+        deal_part(wb_bf, 0, nc.scalar.copy)
         xt3 = tokens(3)
         g1 = gained(1, act1)
         act2 = hidden(2, wa_q, quantise("xt2", xt2))
         quantise_into(g01_q, slice(P, 2 * P), g1[:])
-        deal_half(wb_bf, 1, nc.vector.tensor_copy)
+        deal_part(wb_bf, 1, nc.vector.tensor_copy)
         act3 = hidden(3, wa_q, quantise("xt3", xt3))
         wb_q = quantise("wb", wb_bf)
-        y01 = product_pair(wb_q, g01_q)
+        y01 = product_halves("y01", wb_q, g01_q, 2 * P)
         y2 = product("y2", wb_q, quantise("g2", gained(2, act2)))
-        y3 = product("y3", wb_q, quantise("g3", gained(3, act3)))
-        y01_sb = staged("y_sb01", [P, PACK, 2 * P], F32)
-        for a in range(2):
-            nc.scalar.copy(y01_sb[:, 2 * a : 2 * a + 2, :], y01[a][:])
-        nc.sync.dma_start(y_rows[:, :, 0 : 2 * P], y01_sb[:])
-        stored(2, y2, nc.sync)
+        y3 = product_halves("y3", wb_q, quantise("g3", gained(3, act3)), P)
         y01_bf = staged("y_bf01", [P, 2 * P * PACK], BF16)
         y23_bf = staged("y_bf23", [P, 2 * P * PACK], BF16)
+        y01_sb = staged("y_sb01", [P, PACK, 2 * P], F32)
+        for a in range(2):
+            rows = slice(2 * a, 2 * a + 2)
+            nc.scalar.copy(y01_sb[:, rows, :], y01[a][:])
+            nc.sync.dma_start(y_rows[:, rows, 0 : 2 * P], y01_sb[:, rows, :])
+        y2_sb = stored(2, y2, nc.sync)
+        y3_sb = staged("y_sb3", [P, PACK, P], F32)
+        for a in range(2):
+            nc.scalar.copy(y3_sb[:, 2 * a : 2 * a + 2, :], y3[a][:])
+        nc.scalar.dma_start(y_rows[:, :, 3 * P : 4 * P], y3_sb[:])
         interleave(nc.vector.tensor_copy, y01_bf[:], y01_sb)
-        interleave(nc.scalar.copy, y23_bf[:, 0 : P * PACK], y2)
-        interleave(nc.vector.tensor_copy, y23_bf[:, P * PACK : 2 * P * PACK], y3)
-        stored(3, y3, nc.scalar)
+        interleave(nc.vector.tensor_copy, y23_bf[:, 0 : P * PACK], y2_sb)
         quantise_into(y_q, slice(0, 2 * P), y01_bf[:])
-        store_words(slice(0, 2 * P))
+        interleave(nc.vector.tensor_copy, y23_bf[:, P * PACK : 2 * P * PACK], y3_sb)
         quantise_into(y_q, slice(2 * P, 4 * P), y23_bf[:])
-        store_words(slice(2 * P, 4 * P))
+        store_words(slice(0, 4 * P))
         for q in range(4):
-            store_scales(q, nc.sync)
+            store_scales(q, nc.sync if q < 2 else nc.scalar)

from contextlib import ExitStack

import concourse.mybir as mybir
from concourse.masks import make_identity

E, T, K = 512, 2048, 512
FLOPS = 2 * 2 * 512 * 512 * 512

F32 = mybir.dt.float32
BF16 = mybir.dt.bfloat16
I32 = mybir.dt.int32
U32 = mybir.dt.uint32
U16 = mybir.dt.uint16
U8 = mybir.dt.uint8
FP8X4 = mybir.dt.float8_e4m3fn_x4
GELU = mybir.ActivationFunctionType.Gelu_apprx_tanh
MULT = mybir.AluOpType.mult

P = 128
PACK = 4
HALF = P // 2
BLOCKS = E // P
WB_PARTS = (slice(0, 48), slice(48, P))
PLACE = {"window0":0,"window1":8192,"window2":16384,"window3":24576,"wa_raw":32768,"wb_raw0":40960,"wb_raw1":61440,"wa":0,"xt0_codes":32768,"picked1":3584,"g0":8192,"xt1":49152,"picked2":48640,"picked3":49664,"wb":45056,"g1":24576,"xt2_codes":25600,"xt3":40960,"act2":41984,"xt3_codes":61440,"g2":62464,"g3":57344,"y_bf01":57344,"xt0":4096}
BANK = {"turned0":0,"z0":1,"turned1":2,"z1":3,"turned2":0,"turned3":2,"z2":1,"z3":3,"y01_0":4,"y01_1":5,"y2":6,"y3_0":7,"y3_1":0}


def tile_attend_tokenmixer_pl_kernel(tc, tok, wa, gain, wb, offs, out_0, out_1, out_2):
    nc = tc.nc
    with ExitStack() as ctx:
        keep = ctx.enter_context(tc.tile_pool(name="keep", bufs=1))
        stage = ctx.enter_context(tc.tile_pool(name="stage", bufs=1))
        psum = ctx.enter_context(tc.psum_pool(name="psum", bufs=1))

        def staged(name, shape, dtype):
            if name in PLACE:
                return stage.tile(shape, dtype, name=name, align_bytes=64, offset=PLACE[name])
            return keep.tile(shape, dtype, name=name, align_bytes=64)

        def bank(name, shape):
            return psum.tile(shape, F32, name=name, offset=2048 * BANK[name])

        offsets = keep.tile([P, K // 16], U16, name="offsets")
        gain_sb = keep.tile([P, 1, PACK], F32, name="gain_sb")
        window = [staged("window%d" % b, [P, T], F32) for b in range(BLOCKS)]
        wa_raw = staged("wa_raw", [P, PACK, K], F32)
        wb_raw = [staged("wb_raw%d" % h, [P, PACK, PACK * (WB_PARTS[h].stop - WB_PARTS[h].start)], F32) for h in range(2)]

        nc.sync.dma_start(window[0][:], tok[0:P, :])
        nc.sync.dma_start(offsets[:], offs)
        nc.sync.dma_start(wa_raw[:], wa.rearrange("(p s) c -> p s c", s=PACK))
        nc.scalar.dma_start(gain_sb[:], gain.rearrange("(p t) o -> p o t", t=PACK))
        for b in range(1, BLOCKS):
            nc.sync.dma_start(window[b][:], tok[b * P : (b + 1) * P, :])
        wb_rows = wb.rearrange("(p s) c -> p s c", s=PACK)
        for h in range(2):
            nc.sync.dma_start(wb_raw[h][:], wb_rows[:, :, PACK * WB_PARTS[h].start : PACK * WB_PARTS[h].stop])

        identity = keep.tile([P, P], F32, name="identity")
        make_identity(nc, identity[:])

        def operand(name, width):
            return staged(name + "_codes", [P, width], U32), staged(name + "_scales", [P, width], U8)

        def quantise_into(target, cols, values):
            nc.vector.quantize_mx(
                out=target[0][:, cols].bitcast(FP8X4), scales=target[1][:, cols], in_=values
            )

        def quantise(name, values):
            width = values.shape[1] // PACK
            target = operand(name, width)
            quantise_into(target, slice(0, width), values[:])
            return target

        def deal(name, raw, copy):
            dealt = staged(name, [P, PACK * raw.shape[2]], BF16)
            copy(
                dealt[:].rearrange("p (t m s) -> p m s t", t=PACK, s=PACK),
                raw[:].rearrange("p s (m t) -> p m s t", t=PACK),
            )
            return dealt

        def deal_part(dealt, h, copy):
            copy(
                dealt[:].rearrange("p (t m s) -> p m s t", t=PACK, s=PACK)[:, WB_PARTS[h]],
                wb_raw[h][:].rearrange("p s (m t) -> p m s t", t=PACK),
            )

        def quantise_half(target, h, dealt):
            for t in range(PACK):
                first = t * P + h * HALF
                quantise_into(
                    target, slice(first, first + HALF), dealt[:, t * PACK * HALF : (t + 1) * PACK * HALF]
                )

        def product(name, weights, moving):
            sums = bank(name, [P, PACK, P])
            for t in range(PACK):
                cols = slice(t * P, (t + 1) * P)
                nc.tensor.matmul_mx(
                    out=sums[:, t, :],
                    lhsT=weights[0][:, cols].bitcast(FP8X4),
                    lhsT_scale=weights[1][:, cols],
                    rhs=moving[0][:].bitcast(FP8X4),
                    rhs_scale=moving[1][:],
                    start=True,
                    stop=True,
                )
            return sums

        def tokens(b):
            picked = staged("picked%d" % b, [P, K], BF16)
            nc.vector.tensor_copy(picked[:], window[b][:].indirect(offsets[:]))
            words = picked[:].bitcast(F32)
            turned = bank("turned%d" % b, [P, 2, P])
            for u in range(2):
                nc.tensor.transpose(turned[:, u, :], words[:, u : K // 2 : 2], identity[:])
            xt = staged("xt%d" % b, [P, P * PACK], BF16)
            nc.scalar.copy(
                xt[:].bitcast(F32).rearrange("p (e u) -> p e u", u=2),
                turned[:].rearrange("p u e -> p e u"),
            )
            return xt

        def hidden(b, wa_q, xt_q):
            z = product("z%d" % b, wa_q, xt_q)
            act = staged("act%d" % b, [P, P, PACK], F32)
            nc.scalar.activation(act[:], z[:].rearrange("p t e -> p e t"), GELU)
            return act

        def gained(b, act):
            g = staged("g%d" % b, [P, P * PACK], BF16)
            nc.vector.tensor_tensor(
                g[:].rearrange("p (e t) -> p e t", t=PACK),
                act[:],
                gain_sb[:].to_broadcast([P, P, PACK]),
                MULT,
            )
            return g

        def product_halves(name, weights, moving, width):
            banks = [bank("%s_%d" % (name, a), [P, 2, width]) for a in range(2)]
            for t in range(PACK):
                cols = slice(t * P, (t + 1) * P)
                nc.tensor.matmul_mx(
                    out=banks[t // 2][:, t % 2, :],
                    lhsT=weights[0][:, cols].bitcast(FP8X4),
                    lhsT_scale=weights[1][:, cols],
                    rhs=moving[0][:].bitcast(FP8X4),
                    rhs_scale=moving[1][:],
                    start=True,
                    stop=True,
                )
            return banks

        def interleave(copy, target, y):
            copy(target.rearrange("p (e t) -> p e t", t=PACK), y[:].rearrange("p t e -> p e t"))

        y_q = operand("y", E)
        y_rows = out_0.rearrange("(p t) e -> p t e", t=PACK)
        word_rows = out_1.rearrange("z l c r -> (z l) (c r)").bitcast(I32)
        scale_rows = out_2.rearrange("z q c -> (z q) c").bitcast(I32)

        def stored(b, y, queue):
            y_sb = staged("y_sb%d" % b, [P, PACK, P], F32)
            nc.scalar.copy(y_sb[:], y[:])
            queue.dma_start(y_rows[:, :, b * P : (b + 1) * P], y_sb[:])
            return y_sb

        def rounded(b, y):
            y_bf = staged("y_bf%d" % b, [P, P * PACK], BF16)
            nc.vector.tensor_copy(
                y_bf[:].rearrange("p (e t) -> p e t", t=PACK),
                y[:].rearrange("p t e -> p e t"),
            )
            return y_bf

        def planes(b, y_bf):
            quantise_into(y_q, slice(b * P, (b + 1) * P), y_bf[:])

        def store_words(cols):
            nc.sync.dma_start(word_rows[:, cols], y_q[0][:, cols].bitcast(I32))

        def store_scales(q, queue):
            queue.dma_start(
                scale_rows[4 * q : 4 * q + 4, :], y_q[1][32 * q : 32 * q + 4, :].bitcast(I32)
            )

        xt0 = tokens(0)
        wa_q = quantise("wa", deal("wa", wa_raw, nc.vector.tensor_copy))
        act0 = hidden(0, wa_q, quantise("xt0", xt0))
        xt1 = tokens(1)
        g01_q = operand("g01", 2 * P)
        quantise_into(g01_q, slice(0, P), gained(0, act0)[:])
        act1 = hidden(1, wa_q, quantise("xt1", xt1))
        xt2 = tokens(2)
        wb_bf = staged("wb", [P, PACK * K], BF16)
        deal_part(wb_bf, 0, nc.scalar.copy)
        xt3 = tokens(3)
        g1 = gained(1, act1)
        act2 = hidden(2, wa_q, quantise("xt2", xt2))
        quantise_into(g01_q, slice(P, 2 * P), g1[:])
        deal_part(wb_bf, 1, nc.vector.tensor_copy)
        act3 = hidden(3, wa_q, quantise("xt3", xt3))
        wb_q = quantise("wb", wb_bf)
        y01 = product_halves("y01", wb_q, g01_q, 2 * P)
        y2 = product("y2", wb_q, quantise("g2", gained(2, act2)))
        y3 = product_halves("y3", wb_q, quantise("g3", gained(3, act3)), P)
        y01_bf = staged("y_bf01", [P, 2 * P * PACK], BF16)
        y23_bf = staged("y_bf23", [P, 2 * P * PACK], BF16)
        y01_sb = staged("y_sb01", [P, PACK, 2 * P], F32)
        for a in range(2):
            rows = slice(2 * a, 2 * a + 2)
            nc.scalar.copy(y01_sb[:, rows, :], y01[a][:])
            nc.sync.dma_start(y_rows[:, rows, 0 : 2 * P], y01_sb[:, rows, :])
        y2_sb = stored(2, y2, nc.sync)
        y3_sb = staged("y_sb3", [P, PACK, P], F32)
        for a in range(2):
            nc.scalar.copy(y3_sb[:, 2 * a : 2 * a + 2, :], y3[a][:])
        nc.scalar.dma_start(y_rows[:, :, 3 * P : 4 * P], y3_sb[:])
        interleave(nc.vector.tensor_copy, y01_bf[:], y01_sb)
        interleave(nc.vector.tensor_copy, y23_bf[:, 0 : P * PACK], y2_sb)
        quantise_into(y_q, slice(0, 2 * P), y01_bf[:])
        interleave(nc.vector.tensor_copy, y23_bf[:, P * PACK : 2 * P * PACK], y3_sb)
        quantise_into(y_q, slice(2 * P, 4 * P), y23_bf[:])
        store_words(slice(0, 4 * P))
        for q in range(4):
            store_scales(q, nc.sync if q < 2 else nc.scalar)
